import numpy as np
import ml_dtypes


def mxq(x, axis, fmt="e4m3"):
    dtype, down = {"e4m3": (ml_dtypes.float8_e4m3fn, 7), "e5m2": (ml_dtypes.float8_e5m2, 14)}[fmt]
    v = np.moveaxis(np.asarray(x, np.float32).astype(ml_dtypes.bfloat16).astype(np.float64), axis, -1)
    blocks = v.reshape(v.shape[:-1] + (-1, 32))
    amax = np.abs(blocks).max(-1, keepdims=True)
    byte = np.maximum(np.where(amax > 0, np.frexp(amax)[1] - 1 + 127, 0) - down, 1)
    scale = np.exp2(byte - 127.0)
    codes = (blocks / scale).astype(np.float32).astype(dtype).astype(np.float64)
    return np.moveaxis((codes * scale).reshape(v.shape), -1, axis)


WIDE = False


def mx_kscale(k):
    if not WIDE:
        return np.ones(k)
    levels = np.array([10, -10, 5, -5, 0])
    if k % 512:
        return np.exp2(np.random.permutation(np.resize(levels, k // 32))).repeat(32)
    a = np.empty((k // 512, 16))
    for p in range(k // 512):
        a[p, :8] = np.random.permutation(np.resize(levels, 8))
        for g in range(8):
            far = levels[np.abs(levels - a[p, g]) >= 10]
            a[p, g + 8] = far[np.random.randint(len(far))]
    return np.exp2(a.ravel()).repeat(32)


def f64(x):
    return np.asarray(x).astype(np.float64)


def striped(idx):
    return np.tile(idx.reshape(-1, 16).T, (8, 1)).astype(np.uint16)


def unstriped(offs):
    return offs[:16].T.reshape(-1).astype(np.int64)


def striped8(idx):
    return np.concatenate([x.reshape(-1, 16).T for x in idx]).astype(np.uint16)


def runs(offs, k):
    lists = np.stack([offs[16 * r : 16 * r + 16].T.reshape(-1) for r in range(8)]).astype(np.int64)
    return lists[np.arange(k) % 512 // 64]


def pack_weight(w):
    k, n = w.shape
    w = f64(np.asarray(w, np.float32).astype(ml_dtypes.bfloat16)).reshape(k // 32, 32, n)
    amax = np.abs(w).max(1)
    byte = np.clip(np.where(amax > 0, np.frexp(amax)[1] - 1 + 127 - 7, 1), 1, 254)
    scaled = (w * np.exp2(127.0 - byte)[:, None, :]).reshape(k, n).astype(np.float32)
    words = np.ascontiguousarray(scaled.reshape(k // 512, 128, 4, n).transpose(0, 1, 3, 2)).astype(ml_dtypes.float8_e4m3fn).view(np.uint8)
    return words, np.ascontiguousarray(byte.astype(np.uint8).reshape(k // 512, 16, n))


def unpack_weight(words, scales):
    g, p, n, _ = words.shape
    vals = np.ascontiguousarray(words).view(ml_dtypes.float8_e4m3fn).astype(np.float64) * np.repeat(np.exp2(scales.astype(np.float64) - 127.0), 8, axis=1)[..., None]
    return vals.transpose(0, 1, 3, 2).reshape(g * 512, n)

def planes(y):
    n, m = y.shape
    v = y.astype(np.float32).astype(ml_dtypes.bfloat16).astype(np.float64).reshape(n // 32, 32, m)
    top = np.abs(v).max(1)
    byte = np.clip(np.where(top > 0, np.frexp(top)[1] - 1 + 127 - 7, 1), 1, 254)
    codes = (v * np.exp2(127.0 - byte)[:, None, :]).reshape(n, m).astype(np.float32).astype(ml_dtypes.float8_e4m3fn).view(np.uint8)
    words = codes.reshape(n // 512, 128, 4, m).transpose(0, 1, 3, 2)
    return np.ascontiguousarray(words), np.ascontiguousarray(byte.astype(np.uint8).reshape(n // 512, 16, m))


K, T, S, G, H, W, C = 512, 1024, 256, 2048, 512, 128, 512


def setup_inputs():
    n = np.random.standard_normal
    s = mx_kscale(K)[:, None]
    packed_xT = pack_weight(n((K, T)) * s)
    packed_dT = pack_weight(n((K, G)) / s)
    perm = np.random.permutation(S)
    perm2 = np.random.permutation(S)
    perm3 = np.random.permutation(S)
    return {
        "x_words": packed_xT[0],
        "x_scales": packed_xT[1],
        "d_words": packed_dT[0],
        "d_scales": packed_dT[1],
        "gs": (np.random.uniform(0.5, 1.5, (K, 1)) / s).astype(np.float32),
        "offs": striped(np.random.permutation(T)[:S]),
        "k1": striped8(np.random.randint(0, G, (8, H))),
        "hz": striped8(np.random.randint(0, T, (8, S))),
        "k2": striped8(np.random.randint(0, G, (8, H))),
        "n1": striped(perm[:W]),
        "n2": striped(perm[W:]),
        "n3": striped(perm2[:W]),
        "n4": striped(perm2[W:]),
        "cand": striped8(np.random.randint(0, T, (8, C))),
        "n5": striped(perm3[:W]),
        "n6": striped(perm3[W:]),
        "n7": striped(np.random.permutation(S)),
    }


def reference(x_words, x_scales, d_words, d_scales, gs, offs, k1, hz, k2, n1, n2, n3, n4, cand, n5, n6, n7):
    x_cand = unpack_weight(x_words, x_scales)[np.arange(K)[:, None], runs(cand, K)]
    d_k1 = unpack_weight(d_words, d_scales)[np.arange(K)[:, None], runs(k1, K)]
    xq = unpack_weight(x_words, x_scales)[:, unstriped(offs)]
    d_k2 = unpack_weight(d_words, d_scales)[np.arange(K)[:, None], runs(k2, K)]
    x_hz = unpack_weight(x_words, x_scales)[np.arange(K)[:, None], runs(hz, K)]
    h = 0.0625 * (d_k1.T @ xq + d_k2.T @ x_hz)
    pa = h[:, unstriped(n1)]
    pb = h[:, unstriped(n2)]
    rb = pa - pb
    ra = np.maximum(pa, pb)
    ua = np.zeros((H, S))
    ua[:, unstriped(n3)] = ra
    ub = ua.copy()
    ub[:, unstriped(n4)] = rb
    z = f64(gs) * ub
    s = 0.0625 * ((x_cand.T @ mxq(z, 0, "e4m3")))
    pa2 = s[:, unstriped(n5)]
    pb2 = s[:, unstriped(n6)]
    rb2 = pa2 - pb2
    ua2 = np.zeros((C, S))
    ua2[:, unstriped(n5)] = pb2
    ub2 = ua2.copy()
    ub2[:, unstriped(n6)] = rb2
    out_0 = np.maximum(ub2, 0.5 * ub2[:, unstriped(n7)])
    return (out_0,) + planes(out_0)

@@ -1,0 +1,269 @@
+from contextlib import ExitStack
+
+import concourse.mybir as mybir
+
+K, T, S, G, H, W, C = 512, 1024, 256, 2048, 512, 128, 512
+P = 128
+PACK = 4
+FLOPS = 2 * K * H * S * 2 + 2 * K * C * S
+
+F32 = mybir.dt.float32
+BF16 = mybir.dt.bfloat16
+I32 = mybir.dt.int32
+U32 = mybir.dt.uint32
+U16 = mybir.dt.uint16
+U8 = mybir.dt.uint8
+FP8X4 = mybir.dt.float8_e4m3fn_x4
+ALU = mybir.AluOpType
+COPY = mybir.ActivationFunctionType.Copy
+
+
+def tile_picked_mthzkcpmxswapd_none_po_kernel(
+    tc, x_words, x_scales, d_words, d_scales, gs, offs, k1, hz, k2, n1, n2, n3, n4, cand, n5, n6, n7, out_0, out_1, out_2
+):
+    nc = tc.nc
+    with ExitStack() as ctx:
+        keep = ctx.enter_context(tc.tile_pool(name="keep", bufs=1))
+        psum = ctx.enter_context(tc.psum_pool(name="psum", bufs=1))
+
+        def sb(name, shape, dtype, tag=None):
+            return keep.tile(shape, dtype, name=name, tag=tag or name, align_bytes=64)
+
+        def load_list(name, src):
+            tile = sb(name, list(src.shape), U16)
+            nc.sync.dma_start(tile[:], src)
+            return tile
+
+        d_sc = sb("d_sc", [P, G], U8)
+        x_sc = sb("x_sc", [P, T], U8)
+        placed1 = sb("placed1", [P, 2 * H + 2 * S], U8)
+        placed2 = sb("placed2", [P, C], U8)
+        nc.vector.memset(placed1[:].bitcast(I32), 0)
+        nc.vector.memset(placed2[:].bitcast(I32), 0)
+
+        def load_scales(tile, src):
+            rows = src[0].bitcast(I32)
+            nc.sync.dma_start(tile[:].bitcast(I32), rows.unsqueeze(1).broadcast_to([16, 8, rows.shape[1]]))
+
+        load_scales(x_sc, x_scales)
+        offs_l = load_list("offs_l", offs)
+        hz_l = load_list("hz_l", hz)
+        load_scales(d_sc, d_scales)
+        k1_l = load_list("k1_l", k1)
+        k2_l = load_list("k2_l", k2)
+        x_w = sb("x_w", [P, T], U32)
+        d_w = sb("d_w", [P, G], U32)
+        nc.sync.dma_start(x_w[:].bitcast(I32), x_words[0].rearrange("p n t -> p (n t)").bitcast(I32))
+        nc.sync.dma_start(d_w[:].bitcast(I32), d_words[0].rearrange("p n t -> p (n t)").bitcast(I32))
+        n1_l = load_list("n1_l", n1)
+        n2_l = load_list("n2_l", n2)
+        n3_l = load_list("n3_l", n3)
+        n4_l = load_list("n4_l", n4)
+        gs_sb = sb("gs_sb", [P, PACK], F32)
+        nc.sync.dma_start(gs_sb[:], gs.rearrange("(p t) o -> p (t o)", t=PACK))
+        cand_l = load_list("cand_l", cand)
+        n5_l = load_list("n5_l", n5)
+        n6_l = load_list("n6_l", n6)
+        n7_l = load_list("n7_l", n7)
+
+        def place_scale_rows(placed, picked, queues):
+            for q in range(4):
+                queues[q % len(queues)].dma_start(
+                    placed[32 * q : 32 * q + 4, :].bitcast(I32), picked[32 * q : 32 * q + 32 : 8, :].bitcast(I32)
+                )
+
+        picked1 = sb("picked1", [P, 2 * H + 2 * S], U8, tag="picked1")
+        nc.vector.tensor_copy(picked1[:, 2 * H : 2 * H + S], x_sc[:].indirect(offs_l[:]))
+        nc.vector.tensor_copy(picked1[:, 2 * H + S :], x_sc[:].indirect(hz_l[:]))
+        nc.vector.tensor_copy(picked1[:, 0:H], d_sc[:].indirect(k1_l[:]))
+        nc.vector.tensor_copy(picked1[:, H : 2 * H], d_sc[:].indirect(k2_l[:]))
+        place_scale_rows(placed1, picked1, [nc.scalar, nc.sync])
+
+        xq_w = sb("xq_w", [P, 2, S], U32)
+        nc.vector.tensor_copy(xq_w[:, 0, :], x_w[:].indirect(offs_l[:]))
+        nc.vector.tensor_copy(xq_w[:, 1, :], x_w[:].indirect(hz_l[:]))
+        dk_w = sb("dk_w", [P, 2 * H], U32)
+        nc.vector.tensor_copy(dk_w[:, 0:H], d_w[:].indirect(k1_l[:]))
+        nc.vector.tensor_copy(dk_w[:, H:], d_w[:].indirect(k2_l[:]))
+
+        first_w = sb("first_w", [P, 1, 2 * P], U32)
+        later_w = sb("later_w", [P, PACK - 1, 2 * P], U32, tag="picked1")
+        dealt_s = sb("dealt_s", [P, PACK, 2 * P], U8)
+        dk_by_t = dk_w[:].rearrange("p (m t) -> p t m", t=PACK)
+        sc_by_t = placed1[:, 0 : 2 * H].rearrange("p (m t) -> p t m", t=PACK)
+        h_sb = []
+        for t in range(PACK):
+            words = first_w[:, 0, :] if t == 0 else later_w[:, t - 1, :]
+            nc.vector.tensor_copy(words, dk_by_t[:, t, :])
+            nc.vector.tensor_copy(dealt_s[:, t, :], sc_by_t[:, t, :])
+            acc = psum.tile([P, S], F32, name=f"h_acc{t}")
+            for half in range(2):
+                nc.tensor.matmul_mx(
+                    out=acc[:],
+                    lhsT=words[:, half * P : (half + 1) * P].bitcast(FP8X4),
+                    lhsT_scale=dealt_s[:, t, half * P : (half + 1) * P],
+                    rhs=xq_w[:, half, :].bitcast(FP8X4),
+                    rhs_scale=placed1[:, 2 * H + half * S : 2 * H + (half + 1) * S],
+                    start=(half == 0),
+                    stop=(half == 1),
+                )
+            h_t = sb(f"h{t}", [P, S], F32)
+            if t == 0:
+                nc.scalar.activation(h_t[:], acc[:], COPY, scale=0.0625)
+            else:
+                nc.vector.tensor_scalar(h_t[:], acc[:], 0.0625, None, ALU.mult)
+            h_sb.append(h_t)
+
+        pair = [sb(f"pair{t}", [P, 2, W], F32) for t in range(PACK)]
+        comb = [sb(f"comb{t}", [P, 2, W], F32) for t in range(PACK)]
+        ub = [sb(f"ub{t}", [P, S], F32) for t in range(PACK)]
+        z_bf = sb("z_bf", [P, S, PACK], BF16)
+
+        def fetch_a(t):
+            nc.scalar.activation(pair[t][:, 0, :], h_sb[t][:].indirect(n1_l[:]), COPY)
+
+        def fetch_b(t):
+            nc.scalar.activation(pair[t][:, 1, :], h_sb[t][:].indirect(n2_l[:]), COPY)
+            nc.vector.tensor_tensor(comb[t][:, 0, :], pair[t][:, 0, :], pair[t][:, 1, :], ALU.max)
+            nc.vector.tensor_tensor(comb[t][:, 1, :], pair[t][:, 0, :], pair[t][:, 1, :], ALU.subtract)
+
+        def put_a(t):
+            nc.scalar.activation(ub[t][:].indirect(n3_l[:]), comb[t][:, 0, :], COPY)
+
+        def put_b(t):
+            nc.scalar.activation(ub[t][:].indirect(n4_l[:]), comb[t][:, 1, :], COPY)
+
+        def weigh(t, cols):
+            nc.vector.tensor_scalar(z_bf[:, cols, t], ub[t][:, cols], gs_sb[:, t : t + 1], None, ALU.mult)
+
+        halves = [slice(0, S // 2), slice(S // 2, S)]
+        for t in range(2):
+            fetch_a(t)
+            fetch_b(t)
+        for t in range(2):
+            put_a(t)
+            fetch_a(t + 2)
+            put_b(t)
+            fetch_b(t + 2)
+            weigh(t, slice(0, S))
+
+        picked2 = sb("picked2", [P, C], U8, tag="pair1")
+        nc.vector.tensor_copy(picked2[:], x_sc[:].indirect(cand_l[:]))
+        place_scale_rows(placed2, picked2, [nc.sync])
+        xc_w = sb("xc_w", [P, C], U32, tag="pair2")
+        nc.vector.tensor_copy(xc_w[:], x_w[:].indirect(cand_l[:]))
+        cand_w = sb("cand_w", [P, PACK, P], U32)
+        cand_s = sb("cand_s", [P, PACK, P], U8)
+        nc.vector.tensor_copy(
+            cand_w[:].rearrange("p t (c i) -> p c t i", i=4), xc_w[:].rearrange("p (c i t) -> p c t i", i=4, t=PACK)
+        )
+        nc.vector.tensor_copy(
+            cand_s[:].rearrange("p t (c i) -> p c t i", i=16), placed2[:].rearrange("p (c i t) -> p c t i", i=16, t=PACK)
+        )
+
+        put_a(2)
+        put_a(3)
+        put_b(2)
+        weigh(2, slice(0, S))
+        put_b(3)
+        z_w = sb("z_w", [P, S], U32)
+        z_s = sb("z_s", [P, S], U8)
+        for cols in halves:
+            weigh(3, cols)
+        for cols in halves:
+            nc.vector.quantize_mx(
+                out=z_w[:, cols].bitcast(FP8X4), scales=z_s[:, cols], in_=z_bf[:, cols, :].rearrange("p c t -> p (c t)")
+            )
+
+        s_sb = []
+        for t in range(PACK):
+            s_t = sb(f"s{t}", [P, S], F32)
+            for n, cols in enumerate(halves if t == 0 else [slice(0, S)]):
+                acc = psum.tile([P, cols.stop - cols.start], F32, name=f"s_acc{t}_{n}", tag=f"s_acc{t}" if n == 0 else "h_acc0")
+                nc.tensor.matmul_mx(
+                    out=acc[:],
+                    lhsT=cand_w[:, t, :].bitcast(FP8X4),
+                    lhsT_scale=cand_s[:, t, :],
+                    rhs=z_w[:, cols].bitcast(FP8X4),
+                    rhs_scale=z_s[:, cols],
+                    start=True,
+                    stop=True,
+                )
+                if t == 0:
+                    nc.scalar.activation(s_t[:, cols], acc[:], COPY, scale=0.0625)
+                else:
+                    nc.vector.tensor_scalar(s_t[:], acc[:], 0.0625, None, ALU.mult)
+            s_sb.append(s_t)
+
+        pair2 = [sb(f"pairb{t}", [P, 2, W], F32) for t in range(PACK)]
+        diff2 = [sb(f"diff{t}", [P, W], F32) for t in range(PACK)]
+        ub2 = [sb(f"ubb{t}", [P, S], F32) for t in range(PACK)]
+        other = [sb(f"other{t}", [P, S], F32) for t in range(PACK)]
+        y = sb("y", [P, PACK, S], F32)
+        y_bf = sb("y_bf", [P, S, PACK], BF16)
+        out_rows = out_0.rearrange("(p t) c -> p t c", t=PACK)
+
+        def fetch2_a(t):
+            nc.scalar.activation(pair2[t][:, 0, :], s_sb[t][:].indirect(n5_l[:]), COPY)
+
+        def fetch2_b(t):
+            nc.scalar.activation(pair2[t][:, 1, :], s_sb[t][:].indirect(n6_l[:]), COPY)
+            nc.vector.tensor_tensor(diff2[t][:], pair2[t][:, 0, :], pair2[t][:, 1, :], ALU.subtract)
+
+        def put2_a(t):
+            nc.scalar.activation(ub2[t][:].indirect(n5_l[:]), pair2[t][:, 1, :], COPY)
+
+        def put2_b(t):
+            nc.scalar.activation(ub2[t][:].indirect(n6_l[:]), diff2[t][:], COPY)
+
+        def finish(t, half):
+            cols = halves[half]
+            nc.scalar.activation(other[t][:, cols], ub2[t][:].indirect(n7_l[:, half * 8 : (half + 1) * 8]), COPY)
+            nc.vector.scalar_tensor_tensor(y[:, t, cols], other[t][:, cols], 0.5, ub2[t][:, cols], ALU.mult, ALU.max)
+
+        def round_y(t, cols):
+            nc.vector.tensor_copy(y_bf[:, cols, t], y[:, t, cols])
+
+        def store_y(t, cols):
+            nc.sync.dma_start(out_rows[:, t, cols], y[:, t, cols])
+
+        whole = slice(0, S)
+        y_w = sb("y_w", [P, S], U32)
+        y_s = sb("y_s", [P, S], U8)
+        out_words = out_1[0].rearrange("p n t -> p (n t)").bitcast(I32)
+        for t in range(2):
+            fetch2_a(t)
+            fetch2_b(t)
+        for t in range(2):
+            put2_a(t)
+            fetch2_a(t + 2)
+            put2_b(t)
+            fetch2_b(t + 2)
+        finish(0, 0)
+        put2_a(2)
+        finish(0, 1)
+        store_y(0, whole)
+        round_y(0, whole)
+        put2_b(2)
+        finish(1, 0)
+        finish(1, 1)
+        store_y(1, whole)
+        round_y(1, whole)
+        put2_a(3)
+        finish(2, 0)
+        round_y(2, halves[0])
+        put2_b(3)
+        finish(2, 1)
+        store_y(2, whole)
+        round_y(2, halves[1])
+        for half, cols in enumerate(halves):
+            finish(3, half)
+            round_y(3, cols)
+            nc.vector.quantize_mx(
+                out=y_w[:, cols].bitcast(FP8X4), scales=y_s[:, cols], in_=y_bf[:, cols, :].rearrange("p c t -> p (c t)")
+            )
+            store_y(3, cols)
+            nc.sync.dma_start(out_words[:, cols], y_w[:, cols].bitcast(I32))
+        for q in range(4):
+            queue = nc.scalar if q % 4 != 3 else nc.sync
+            queue.dma_start(out_2[0, 4 * q : 4 * q + 4, :].bitcast(I32), y_s[32 * q : 32 * q + 4, :].bitcast(I32))

@@ -55,17 +55,6 @@ def tile_picked_mthzkcpmxswapd_none_po_kernel(
         d_w = sb("d_w", [P, G], U32)
         nc.sync.dma_start(x_w[:].bitcast(I32), x_words[0].rearrange("p n t -> p (n t)").bitcast(I32))
         nc.sync.dma_start(d_w[:].bitcast(I32), d_words[0].rearrange("p n t -> p (n t)").bitcast(I32))
-        n1_l = load_list("n1_l", n1)
-        n2_l = load_list("n2_l", n2)
-        n3_l = load_list("n3_l", n3)
-        n4_l = load_list("n4_l", n4)
-        gs_sb = sb("gs_sb", [P, PACK], F32)
-        nc.sync.dma_start(gs_sb[:], gs.rearrange("(p t) o -> p (t o)", t=PACK))
-        cand_l = load_list("cand_l", cand)
-        n5_l = load_list("n5_l", n5)
-        n6_l = load_list("n6_l", n6)
-        n7_l = load_list("n7_l", n7)
-
         def place_scale_rows(placed, picked, queues):
             for q in range(4):
                 queues[q % len(queues)].dma_start(
@@ -78,6 +67,17 @@ def tile_picked_mthzkcpmxswapd_none_po_kernel(
         nc.vector.tensor_copy(picked1[:, 0:H], d_sc[:].indirect(k1_l[:]))
         nc.vector.tensor_copy(picked1[:, H : 2 * H], d_sc[:].indirect(k2_l[:]))
         place_scale_rows(placed1, picked1, [nc.scalar, nc.sync])
+
+        n1_l = load_list("n1_l", n1)
+        n2_l = load_list("n2_l", n2)
+        n3_l = load_list("n3_l", n3)
+        n4_l = load_list("n4_l", n4)
+        gs_sb = sb("gs_sb", [P, PACK], F32)
+        nc.gpsimd.dma_start(gs_sb[:], gs.rearrange("(p t) o -> p (t o)", t=PACK))
+        cand_l = load_list("cand_l", cand)
+        n5_l = load_list("n5_l", n5)
+        n6_l = load_list("n6_l", n6)
+        n7_l = load_list("n7_l", n7)
 
         xq_w = sb("xq_w", [P, 2, S], U32)
         nc.vector.tensor_copy(xq_w[:, 0, :], x_w[:].indirect(offs_l[:]))
@@ -117,7 +117,6 @@ def tile_picked_mthzkcpmxswapd_none_po_kernel(
         pair = [sb(f"pair{t}", [P, 2, W], F32) for t in range(PACK)]
         comb = [sb(f"comb{t}", [P, 2, W], F32) for t in range(PACK)]
         ub = [sb(f"ub{t}", [P, S], F32) for t in range(PACK)]
-        z_bf = sb("z_bf", [P, S, PACK], BF16)
 
         def fetch_a(t):
             nc.scalar.activation(pair[t][:, 0, :], h_sb[t][:].indirect(n1_l[:]), COPY)
@@ -145,7 +144,6 @@ def tile_picked_mthzkcpmxswapd_none_po_kernel(
             fetch_a(t + 2)
             put_b(t)
             fetch_b(t + 2)
-            weigh(t, slice(0, S))
 
         picked2 = sb("picked2", [P, C], U8, tag="pair1")
         nc.vector.tensor_copy(picked2[:], x_sc[:].indirect(cand_l[:]))
@@ -161,6 +159,9 @@ def tile_picked_mthzkcpmxswapd_none_po_kernel(
             cand_s[:].rearrange("p t (c i) -> p c t i", i=16), placed2[:].rearrange("p (c i t) -> p c t i", i=16, t=PACK)
         )
 
+        z_bf = sb("z_bf", [P, S, PACK], BF16, tag="placed2")
+        weigh(0, slice(0, S))
+        weigh(1, slice(0, S))
         put_a(2)
         put_a(3)
         put_b(2)

@@ -73,7 +73,7 @@ def tile_picked_mthzkcpmxswapd_none_po_kernel(
         n3_l = load_list("n3_l", n3)
         n4_l = load_list("n4_l", n4)
         gs_sb = sb("gs_sb", [P, PACK], F32)
-        nc.gpsimd.dma_start(gs_sb[:], gs.rearrange("(p t) o -> p (t o)", t=PACK))
+        nc.sync.dma_start(gs_sb[:], gs.rearrange("(p t) o -> p (t o)", t=PACK))
         cand_l = load_list("cand_l", cand)
         n5_l = load_list("n5_l", n5)
         n6_l = load_list("n6_l", n6)
@@ -217,9 +217,8 @@ def tile_picked_mthzkcpmxswapd_none_po_kernel(
         def put2_b(t):
             nc.scalar.activation(ub2[t][:].indirect(n6_l[:]), diff2[t][:], COPY)
 
-        def finish(t, half):
-            cols = halves[half]
-            nc.scalar.activation(other[t][:, cols], ub2[t][:].indirect(n7_l[:, half * 8 : (half + 1) * 8]), COPY)
+        def finish(t, cols):
+            nc.scalar.activation(other[t][:, cols], ub2[t][:].indirect(n7_l[:, cols.start // 16 : cols.stop // 16]), COPY)
             nc.vector.scalar_tensor_tensor(y[:, t, cols], other[t][:, cols], 0.5, ub2[t][:, cols], ALU.mult, ALU.max)
 
         def round_y(t, cols):
@@ -240,31 +239,33 @@ def tile_picked_mthzkcpmxswapd_none_po_kernel(
             fetch2_a(t + 2)
             put2_b(t)
             fetch2_b(t + 2)
-        finish(0, 0)
+        finish(0, halves[0])
         put2_a(2)
-        finish(0, 1)
+        finish(0, halves[1])
         store_y(0, whole)
         round_y(0, whole)
         put2_b(2)
-        finish(1, 0)
-        finish(1, 1)
+        finish(1, halves[0])
+        finish(1, halves[1])
         store_y(1, whole)
         round_y(1, whole)
         put2_a(3)
-        finish(2, 0)
+        finish(2, halves[0])
         round_y(2, halves[0])
         put2_b(3)
-        finish(2, 1)
+        finish(2, halves[1])
         store_y(2, whole)
         round_y(2, halves[1])
-        for half, cols in enumerate(halves):
-            finish(3, half)
+        for cols in (slice(0, 128), slice(128, 192), slice(192, 256)):
+            finish(3, cols)
             round_y(3, cols)
             nc.vector.quantize_mx(
                 out=y_w[:, cols].bitcast(FP8X4), scales=y_s[:, cols], in_=y_bf[:, cols, :].rearrange("p c t -> p (c t)")
             )
-            store_y(3, cols)
-            nc.sync.dma_start(out_words[:, cols], y_w[:, cols].bitcast(I32))
+            if cols.stop != 192:
+                done = halves[cols.start // 128]
+                store_y(3, done)
+                nc.sync.dma_start(out_words[:, done], y_w[:, done].bitcast(I32))
         for q in range(4):
             queue = nc.scalar if q % 4 != 3 else nc.sync
             queue.dma_start(out_2[0, 4 * q : 4 * q + 4, :].bitcast(I32), y_s[32 * q : 32 * q + 4, :].bitcast(I32))

from contextlib import ExitStack

import concourse.mybir as mybir

K, T, S, G, H, W, C = 512, 1024, 256, 2048, 512, 128, 512
P = 128
PACK = 4
FLOPS = 2 * K * H * S * 2 + 2 * K * C * S

F32 = mybir.dt.float32
BF16 = mybir.dt.bfloat16
I32 = mybir.dt.int32
U32 = mybir.dt.uint32
U16 = mybir.dt.uint16
U8 = mybir.dt.uint8
FP8X4 = mybir.dt.float8_e4m3fn_x4
ALU = mybir.AluOpType
COPY = mybir.ActivationFunctionType.Copy


def tile_picked_mthzkcpmxswapd_none_po_kernel(
    tc, x_words, x_scales, d_words, d_scales, gs, offs, k1, hz, k2, n1, n2, n3, n4, cand, n5, n6, n7, out_0, out_1, out_2
):
    nc = tc.nc
    with ExitStack() as ctx:
        keep = ctx.enter_context(tc.tile_pool(name="keep", bufs=1))
        psum = ctx.enter_context(tc.psum_pool(name="psum", bufs=1))

        def sb(name, shape, dtype, tag=None):
            return keep.tile(shape, dtype, name=name, tag=tag or name, align_bytes=64)

        def load_list(name, src):
            tile = sb(name, list(src.shape), U16)
            nc.sync.dma_start(tile[:], src)
            return tile

        d_sc = sb("d_sc", [P, G], U8)
        x_sc = sb("x_sc", [P, T], U8)
        placed1 = sb("placed1", [P, 2 * H + 2 * S], U8)
        placed2 = sb("placed2", [P, C], U8)
        nc.vector.memset(placed1[:].bitcast(I32), 0)
        nc.vector.memset(placed2[:].bitcast(I32), 0)

        def load_scales(tile, src):
            rows = src[0].bitcast(I32)
            nc.sync.dma_start(tile[:].bitcast(I32), rows.unsqueeze(1).broadcast_to([16, 8, rows.shape[1]]))

        load_scales(x_sc, x_scales)
        offs_l = load_list("offs_l", offs)
        hz_l = load_list("hz_l", hz)
        load_scales(d_sc, d_scales)
        k1_l = load_list("k1_l", k1)
        k2_l = load_list("k2_l", k2)
        x_w = sb("x_w", [P, T], U32)
        d_w = sb("d_w", [P, G], U32)
        nc.sync.dma_start(x_w[:].bitcast(I32), x_words[0].rearrange("p n t -> p (n t)").bitcast(I32))
        nc.sync.dma_start(d_w[:].bitcast(I32), d_words[0].rearrange("p n t -> p (n t)").bitcast(I32))
        def place_scale_rows(placed, picked, queues):
            for q in range(4):
                queues[q % len(queues)].dma_start(
                    placed[32 * q : 32 * q + 4, :].bitcast(I32), picked[32 * q : 32 * q + 32 : 8, :].bitcast(I32)
                )

        picked1 = sb("picked1", [P, 2 * H + 2 * S], U8, tag="picked1")
        nc.vector.tensor_copy(picked1[:, 2 * H : 2 * H + S], x_sc[:].indirect(offs_l[:]))
        nc.vector.tensor_copy(picked1[:, 2 * H + S :], x_sc[:].indirect(hz_l[:]))
        nc.vector.tensor_copy(picked1[:, 0:H], d_sc[:].indirect(k1_l[:]))
        nc.vector.tensor_copy(picked1[:, H : 2 * H], d_sc[:].indirect(k2_l[:]))
        place_scale_rows(placed1, picked1, [nc.scalar, nc.sync])

        n1_l = load_list("n1_l", n1)
        n2_l = load_list("n2_l", n2)
        n3_l = load_list("n3_l", n3)
        n4_l = load_list("n4_l", n4)
        gs_sb = sb("gs_sb", [P, PACK], F32)
        nc.sync.dma_start(gs_sb[:], gs.rearrange("(p t) o -> p (t o)", t=PACK))
        cand_l = load_list("cand_l", cand)
        n5_l = load_list("n5_l", n5)
        n6_l = load_list("n6_l", n6)
        n7_l = load_list("n7_l", n7)

        xq_w = sb("xq_w", [P, 2, S], U32)
        nc.vector.tensor_copy(xq_w[:, 0, :], x_w[:].indirect(offs_l[:]))
        nc.vector.tensor_copy(xq_w[:, 1, :], x_w[:].indirect(hz_l[:]))
        dk_w = sb("dk_w", [P, 2 * H], U32)
        nc.vector.tensor_copy(dk_w[:, 0:H], d_w[:].indirect(k1_l[:]))
        nc.vector.tensor_copy(dk_w[:, H:], d_w[:].indirect(k2_l[:]))

        first_w = sb("first_w", [P, 1, 2 * P], U32)
        later_w = sb("later_w", [P, PACK - 1, 2 * P], U32, tag="picked1")
        dealt_s = sb("dealt_s", [P, PACK, 2 * P], U8)
        dk_by_t = dk_w[:].rearrange("p (m t) -> p t m", t=PACK)
        sc_by_t = placed1[:, 0 : 2 * H].rearrange("p (m t) -> p t m", t=PACK)
        h_sb = []
        for t in range(PACK):
            words = first_w[:, 0, :] if t == 0 else later_w[:, t - 1, :]
            nc.vector.tensor_copy(words, dk_by_t[:, t, :])
            nc.vector.tensor_copy(dealt_s[:, t, :], sc_by_t[:, t, :])
            acc = psum.tile([P, S], F32, name=f"h_acc{t}")
            for half in range(2):
                nc.tensor.matmul_mx(
                    out=acc[:],
                    lhsT=words[:, half * P : (half + 1) * P].bitcast(FP8X4),
                    lhsT_scale=dealt_s[:, t, half * P : (half + 1) * P],
                    rhs=xq_w[:, half, :].bitcast(FP8X4),
                    rhs_scale=placed1[:, 2 * H + half * S : 2 * H + (half + 1) * S],
                    start=(half == 0),
                    stop=(half == 1),
                )
            h_t = sb(f"h{t}", [P, S], F32)
            if t == 0:
                nc.scalar.activation(h_t[:], acc[:], COPY, scale=0.0625)
            else:
                nc.vector.tensor_scalar(h_t[:], acc[:], 0.0625, None, ALU.mult)
            h_sb.append(h_t)

        pair = [sb(f"pair{t}", [P, 2, W], F32) for t in range(PACK)]
        comb = [sb(f"comb{t}", [P, 2, W], F32) for t in range(PACK)]
        ub = [sb(f"ub{t}", [P, S], F32) for t in range(PACK)]

        def fetch_a(t):
            nc.scalar.activation(pair[t][:, 0, :], h_sb[t][:].indirect(n1_l[:]), COPY)

        def fetch_b(t):
            nc.scalar.activation(pair[t][:, 1, :], h_sb[t][:].indirect(n2_l[:]), COPY)
            nc.vector.tensor_tensor(comb[t][:, 0, :], pair[t][:, 0, :], pair[t][:, 1, :], ALU.max)
            nc.vector.tensor_tensor(comb[t][:, 1, :], pair[t][:, 0, :], pair[t][:, 1, :], ALU.subtract)

        def put_a(t):
            nc.scalar.activation(ub[t][:].indirect(n3_l[:]), comb[t][:, 0, :], COPY)

        def put_b(t):
            nc.scalar.activation(ub[t][:].indirect(n4_l[:]), comb[t][:, 1, :], COPY)

        def weigh(t, cols):
            nc.vector.tensor_scalar(z_bf[:, cols, t], ub[t][:, cols], gs_sb[:, t : t + 1], None, ALU.mult)

        halves = [slice(0, S // 2), slice(S // 2, S)]
        for t in range(2):
            fetch_a(t)
            fetch_b(t)
        for t in range(2):
            put_a(t)
            fetch_a(t + 2)
            put_b(t)
            fetch_b(t + 2)

        picked2 = sb("picked2", [P, C], U8, tag="pair1")
        nc.vector.tensor_copy(picked2[:], x_sc[:].indirect(cand_l[:]))
        place_scale_rows(placed2, picked2, [nc.sync])
        xc_w = sb("xc_w", [P, C], U32, tag="pair2")
        nc.vector.tensor_copy(xc_w[:], x_w[:].indirect(cand_l[:]))
        cand_w = sb("cand_w", [P, PACK, P], U32)
        cand_s = sb("cand_s", [P, PACK, P], U8)
        nc.vector.tensor_copy(
            cand_w[:].rearrange("p t (c i) -> p c t i", i=4), xc_w[:].rearrange("p (c i t) -> p c t i", i=4, t=PACK)
        )
        nc.vector.tensor_copy(
            cand_s[:].rearrange("p t (c i) -> p c t i", i=16), placed2[:].rearrange("p (c i t) -> p c t i", i=16, t=PACK)
        )

        z_bf = sb("z_bf", [P, S, PACK], BF16, tag="placed2")
        weigh(0, slice(0, S))
        weigh(1, slice(0, S))
        put_a(2)
        put_a(3)
        put_b(2)
        weigh(2, slice(0, S))
        put_b(3)
        z_w = sb("z_w", [P, S], U32)
        z_s = sb("z_s", [P, S], U8)
        for cols in halves:
            weigh(3, cols)
        for cols in halves:
            nc.vector.quantize_mx(
                out=z_w[:, cols].bitcast(FP8X4), scales=z_s[:, cols], in_=z_bf[:, cols, :].rearrange("p c t -> p (c t)")
            )

        s_sb = []
        for t in range(PACK):
            s_t = sb(f"s{t}", [P, S], F32)
            for n, cols in enumerate(halves if t == 0 else [slice(0, S)]):
                acc = psum.tile([P, cols.stop - cols.start], F32, name=f"s_acc{t}_{n}", tag=f"s_acc{t}" if n == 0 else "h_acc0")
                nc.tensor.matmul_mx(
                    out=acc[:],
                    lhsT=cand_w[:, t, :].bitcast(FP8X4),
                    lhsT_scale=cand_s[:, t, :],
                    rhs=z_w[:, cols].bitcast(FP8X4),
                    rhs_scale=z_s[:, cols],
                    start=True,
                    stop=True,
                )
                if t == 0:
                    nc.scalar.activation(s_t[:, cols], acc[:], COPY, scale=0.0625)
                else:
                    nc.vector.tensor_scalar(s_t[:], acc[:], 0.0625, None, ALU.mult)
            s_sb.append(s_t)

        pair2 = [sb(f"pairb{t}", [P, 2, W], F32) for t in range(PACK)]
        diff2 = [sb(f"diff{t}", [P, W], F32) for t in range(PACK)]
        ub2 = [sb(f"ubb{t}", [P, S], F32) for t in range(PACK)]
        other = [sb(f"other{t}", [P, S], F32) for t in range(PACK)]
        y = sb("y", [P, PACK, S], F32)
        y_bf = sb("y_bf", [P, S, PACK], BF16)
        out_rows = out_0.rearrange("(p t) c -> p t c", t=PACK)

        def fetch2_a(t):
            nc.scalar.activation(pair2[t][:, 0, :], s_sb[t][:].indirect(n5_l[:]), COPY)

        def fetch2_b(t):
            nc.scalar.activation(pair2[t][:, 1, :], s_sb[t][:].indirect(n6_l[:]), COPY)
            nc.vector.tensor_tensor(diff2[t][:], pair2[t][:, 0, :], pair2[t][:, 1, :], ALU.subtract)

        def put2_a(t):
            nc.scalar.activation(ub2[t][:].indirect(n5_l[:]), pair2[t][:, 1, :], COPY)

        def put2_b(t):
            nc.scalar.activation(ub2[t][:].indirect(n6_l[:]), diff2[t][:], COPY)

        def finish(t, cols):
            nc.scalar.activation(other[t][:, cols], ub2[t][:].indirect(n7_l[:, cols.start // 16 : cols.stop // 16]), COPY)
            nc.vector.scalar_tensor_tensor(y[:, t, cols], other[t][:, cols], 0.5, ub2[t][:, cols], ALU.mult, ALU.max)

        def round_y(t, cols):
            nc.vector.tensor_copy(y_bf[:, cols, t], y[:, t, cols])

        def store_y(t, cols):
            nc.sync.dma_start(out_rows[:, t, cols], y[:, t, cols])

        whole = slice(0, S)
        y_w = sb("y_w", [P, S], U32)
        y_s = sb("y_s", [P, S], U8)
        out_words = out_1[0].rearrange("p n t -> p (n t)").bitcast(I32)
        for t in range(2):
            fetch2_a(t)
            fetch2_b(t)
        for t in range(2):
            put2_a(t)
            fetch2_a(t + 2)
            put2_b(t)
            fetch2_b(t + 2)
        finish(0, halves[0])
        put2_a(2)
        finish(0, halves[1])
        store_y(0, whole)
        round_y(0, whole)
        put2_b(2)
        finish(1, halves[0])
        finish(1, halves[1])
        store_y(1, whole)
        round_y(1, whole)
        put2_a(3)
        finish(2, halves[0])
        round_y(2, halves[0])
        put2_b(3)
        finish(2, halves[1])
        store_y(2, whole)
        round_y(2, halves[1])
        for cols in (slice(0, 128), slice(128, 192), slice(192, 256)):
            finish(3, cols)
            round_y(3, cols)
            nc.vector.quantize_mx(
                out=y_w[:, cols].bitcast(FP8X4), scales=y_s[:, cols], in_=y_bf[:, cols, :].rearrange("p c t -> p (c t)")
            )
            if cols.stop != 192:
                done = halves[cols.start // 128]
                store_y(3, done)
                nc.sync.dma_start(out_words[:, done], y_w[:, done].bitcast(I32))
        for q in range(4):
            queue = nc.scalar if q % 4 != 3 else nc.sync
            queue.dma_start(out_2[0, 4 * q : 4 * q + 4, :].bitcast(I32), y_s[32 * q : 32 * q + 4, :].bitcast(I32))
